import numpy as np, ml_dtypes
CORES = [33,161,289,417,57,185,313,441]
N = 8
T, CAP = 4096, 256
def entries(a): return a.T.reshape(-1)
def pack(v, P): return np.ascontiguousarray(np.asarray(v, np.int32).reshape(-1, P).T)
def lists(rng, how):
    L = rng.integers(0, T, (N, N, CAP))
    if how == "alike": L[:] = rng.integers(0, T, (N, N, 1))
    if how == "distinct": L = np.stack([np.stack([rng.permutation(T)[:CAP] for d in range(N)]) for r in range(N)])
    if how == "sorted": L = np.sort(L, axis=2)
    if how == "edge": L = np.where(rng.random((N, N, CAP)) < 0.5, 0, T - 1)
    return {"l": np.stack([pack(L[r].reshape(-1), 16) for r in range(N)])}
def setup_inputs(rng):
    return dict({"x": rng.standard_normal((N, 128, T), dtype=np.float32).astype(ml_dtypes.bfloat16)}, **lists(rng, "uniform"))
def setup_inputs_alike(rng):
    d = setup_inputs(rng); d.update(lists(rng, "alike"))
    for k in ("x",): d[k] = (d[k].astype(np.float32) * 1048576.0).astype(d[k].dtype)
    return d
def setup_inputs_distinct(rng):
    d = setup_inputs(rng); d.update(lists(rng, "distinct"))
    for k in ("x",): d[k] = (d[k].astype(np.float32) * (1 / 1024.0)).astype(d[k].dtype)
    return d
def setup_inputs_edge(rng):
    d = setup_inputs(rng); d.update(lists(rng, "edge"))
    return d
def setup_inputs_sorted(rng):
    d = setup_inputs(rng); d.update(lists(rng, "sorted"))
    return d
def check_inputs(x):
    bad = []
    if x["l"].min() < 0 or x["l"].max() >= T: bad.append("l out of range")
    return bad
def reference(x, l):
    y = np.zeros((N, 128, N * CAP), x.dtype)
    for r in range(N):
        L = entries(l[r])
        for d in range(N): y[d][:, CAP * r:CAP * r + CAP] = x[r][:, L[CAP * d:CAP * d + CAP]]
    return {"y": y}

@@ -1,0 +1,170 @@
+from concourse.bass import DstId, RemoteDMATransfer
+from concourse.mybir import AluOpType, ActivationFunctionType
+
+N, COLS, W, LP = 8, 4096, 256, 16
+LC = W // LP
+WORLD = 512
+
+SCRATCH = {
+    "xs": ("sbuf", [128, COLS], "bfloat16"),
+    "li": ("sbuf", [128, N * LC], "int32"),
+    "lf": ("sbuf", [128, N * LC], "float32"),
+    "rep": ("sbuf", [128, 128], "float32"),
+    "ps": ("psum", [128, N * LC], "float32"),
+    "off": ("sbuf", [128, N * LC], "uint16"),
+    "snd": ("sbuf", [128, N * W], "bfloat16"),
+    "rly": ("dram", [128, W], "bfloat16"),
+    "land": ("dram", [N, 128, W], "bfloat16"),
+}
+SEMAPHORES = (["lsem", "xsem", "one", "rsel", "lfs", "mm", "offs", "rin", "sent", "st1", "st2"]
+              + ["g%d" % i for i in range(N)] + ["a%d" % i for i in range(N)])
+
+ROUNDS = (("x_same", "x_turn"), ("t_far", "t_rack"), ("t_host", "near"), ("far", "own"))
+STORE_SYNC = ("near", "x_same", "t_rack", "t_host")
+STORE_SCALAR = ("own", "far", "x_turn", "t_far")
+
+_CACHE = {}
+
+
+def _bits(mask):
+    return [1 << i for i in range(mask.bit_length()) if mask >> i & 1]
+
+
+def _count(mask):
+    return len(_bits(mask))
+
+
+def _plan(ranks, topo):
+    if "way" in _CACHE:
+        return _CACHE["way"], _CACHE["job"]
+
+    def same_chip(a, b):
+        return topo.host(a) == topo.host(b) and topo.chip(a) == topo.chip(b)
+
+    def same_rack(a, b):
+        return topo.rack(topo.host(a)) == topo.rack(topo.host(b))
+
+    free = [c for c in range(WORLD) if c not in ranks and any(same_chip(c, r) for r in ranks)]
+    turns = {c: any(topo.mates(c, m) and topo.may_write(c, m) for m in range(WORLD)) for c in free}
+
+    kind = {}
+    for s in ranks:
+        for d in ranks:
+            if s == d:
+                continue
+            if topo.may_write(s, d):
+                kind[s, d] = "near" if topo.same_plane(s, d) else "far"
+            elif any(same_chip(c, s) and topo.may_write(c, d) for c in free):
+                kind[s, d] = "t_host" if topo.host(s) == topo.host(d) else "t_rack" if same_rack(s, d) else "t_far"
+            else:
+                kind[s, d] = "x_same" if topo.chip(s) == topo.chip(d) else "x_turn"
+
+    fits = {
+        "t_host": lambda c, s, d: same_chip(c, s) and topo.die(c) == topo.die(s),
+        "t_far": lambda c, s, d: same_chip(c, s) and topo.die(c) == topo.die(s),
+        "t_rack": lambda c, s, d: same_chip(c, s) and topo.die(c) != topo.die(s),
+        "x_turn": lambda c, s, d: (topo.chip(c) == topo.chip(s) and not same_rack(c, s) and same_rack(c, d)
+                                   and topo.die(c) != topo.die(s)),
+        "x_same": lambda c, s, d: (topo.chip(c) == topo.chip(s) and topo.same_plane(c, s) and not turns[c]
+                                   and topo.die(c) == topo.die(s)),
+    }
+    way, job = {}, {}
+    for k in ("near", "far", "t_host", "t_far", "t_rack", "x_turn", "x_same"):
+        for (s, d), kk in sorted(kind.items()):
+            if kk != k:
+                continue
+            h = None
+            if k in fits:
+                h = [c for c in free if fits[k](c, s, d) and topo.may_write(s, c) and topo.may_write(c, d)][0]
+                free.remove(h)
+                job[h] = (s, d)
+            way[s, d] = (k, h)
+    for (s, d), (k, h) in sorted(way.items()):
+        first = d if h is None else h
+        out = _bits([topo.mask(s, x) for x in ranks if x != s and topo.may_write(s, x)][0])
+        if same_chip(first, s):
+            mine = [b for b in _bits(topo.mask(s, first)) if b not in out]
+            m1 = mine if k == "t_host" else mine[0::2] if k == "t_rack" else mine[1::2]
+        else:
+            m1 = out[0::2] if k in ("x_same", "near") else out[1::2]
+        m2 = _bits(topo.mask(h, d))[0::2] if h is not None else []
+        way[s, d] = (k, h, sum(m1), sum(m2))
+    _CACHE["way"], _CACHE["job"] = way, job
+    return way, job
+
+
+def rank_program(g, core, T, topo):
+    ranks = list(T.cores)
+    way, job = _plan(ranks, topo)
+    sem = T.sem
+
+    if core in job:
+        s, d = job[core]
+        _, _, m1, m2 = way[s, d]
+        rs = T.rank_of(s)
+        rid, pid = topo.addr(d, core)
+        g.wait_ge(sem.rin, _count(m1))
+        g.remote_dma(T.land[rs], T.rly[:, :], sem["a%d" % rs], sem.sent, pid, rid, m2)
+        g.wait_ge(sem.sent, _count(m2))
+        return
+
+    r = T.rank_of(core)
+    if r is None:
+        return
+    to = {way[core, d][0]: d for d in ranks if d != core}
+    frm = {way[s, core][0]: s for s in ranks if s != core}
+    to["own"] = frm["own"] = core
+
+    g.sync.dma_start(T.li[0:LP, :], T.l[:, :]).then_inc(sem.lsem, 16)
+    g.sync.dma_start(T.xs[:, :], T.x[:, :]).then_inc(sem.xsem, 16)
+    g.vector.memset(T.rep[0:LP, :], 1.0).then_inc(sem.one, 1)
+    g.wait_ge(sem.one, 1)
+    g.affine_select(T.rep[0:LP, :], T.rep[0:LP, :], [[0, 128 // LP], [-1, LP]], AluOpType.is_equal, 0.0, 0, 1).then_inc(sem.rsel, 1)
+    g.vector.wait_ge(sem.lsem, 16)
+    g.vector.tensor_copy(T.lf[0:LP, :], T.li[0:LP, :]).then_inc(sem.lfs, 1)
+    g.tensor.wait_ge(sem.rsel, 1)
+    g.tensor.wait_ge(sem.lfs, 1)
+    g.tensor.matmul(T.ps[:, :], T.rep[0:LP, :], T.lf[0:LP, :], True, True).then_inc(sem.mm, 1)
+    g.vector.wait_ge(sem.mm, 1)
+    g.vector.tensor_copy(T.off[:, :], T.ps[:, :]).then_inc(sem.offs, 1)
+    for q in (g.vector, g.scalar):
+        q.wait_ge(sem.offs, 1)
+        q.wait_ge(sem.xsem, 16)
+
+    sent = 0
+    for row in ROUNDS:
+        transfers = []
+        for i, k in enumerate(row):
+            rd = T.rank_of(to[k])
+            blk = T.snd[:, rd * W:(rd + 1) * W]
+            win = T.xs[:, 0:COLS].indirect(T.off[:, rd * LC:(rd + 1) * LC])
+            if i == 0:
+                g.vector.tensor_copy(blk, win).then_inc(sem["g%d" % rd], 1)
+            else:
+                g.scalar.activation(blk, win, ActivationFunctionType.Copy).then_inc(sem["g%d" % rd], 1)
+            if k == "own":
+                continue
+            _, h, m1, _ = way[core, to[k]]
+            g.wait_ge(sem["g%d" % rd], 1)
+            first = to[k] if h is None else h
+            rid, pid = topo.addr(first, core)
+            transfers.append(RemoteDMATransfer(
+                dst_ids=[DstId(rid=rid, pnc=pid)], dma_engine_mask=m1,
+                remote_sem=sem["a%d" % r] if h is None else sem.rin,
+                src=blk, dst=T.land[r] if h is None else T.rly[:, :]))
+            sent += _count(m1)
+        g.remote_dma_fused(transfers, local_sem=sem.sent)
+
+    for q, order, st in ((g.sync, STORE_SYNC, sem.st1), (g.scalar, STORE_SCALAR, sem.st2)):
+        for k in order:
+            rs = T.rank_of(frm[k])
+            if k == "own":
+                q.wait_ge(sem["g%d" % rs], 1)
+                src = T.snd[:, rs * W:(rs + 1) * W]
+            else:
+                _, h, m1, m2 = way[frm[k], core]
+                q.wait_ge(sem["a%d" % rs], _count(m1 if h is None else m2))
+                src = T.land[rs]
+            q.dma_start(T.y[:, rs * W:(rs + 1) * W], src).then_inc(st, 16)
+        q.wait_ge(st, 16 * len(order))
+    g.wait_ge(sem.sent, sent)

@@ -13,15 +13,16 @@ SCRATCH = {
     "ps": ("psum", [128, N * LC], "float32"),
     "off": ("sbuf", [128, N * LC], "uint16"),
     "snd": ("sbuf", [128, N * W], "bfloat16"),
-    "rly": ("dram", [128, W], "bfloat16"),
+    "rly": ("dram", [3, 128, W], "bfloat16"),
     "land": ("dram", [N, 128, W], "bfloat16"),
 }
-SEMAPHORES = (["lsem", "xsem", "one", "rsel", "lfs", "mm", "offs", "rin", "sent", "st1", "st2"]
+SEMAPHORES = (["lsem", "xsem", "one", "rsel", "lfs", "mm", "offs", "rin0", "rin1", "rin2", "sent", "st1", "st2"]
               + ["g%d" % i for i in range(N)] + ["a%d" % i for i in range(N)])
 
-ROUNDS = (("x_same", "x_turn"), ("t_far", "t_rack"), ("t_host", "near"), ("far", "own"))
-STORE_SYNC = ("near", "x_same", "t_rack", "t_host")
-STORE_SCALAR = ("own", "far", "x_turn", "t_far")
+ROUNDS = (("x_same", "t_far"), ("x_turn", "t_rack"), ("t_host", "near"), ("far", "own"))
+CALLS = (("x_same", "t_far"), ("x_turn", "t_rack"), ("t_host", "near", "far"))
+STORE_SYNC = ("x_same", "near", "t_rack", "t_host")
+STORE_SCALAR = ("t_far", "own", "far", "x_turn")
 
 _CACHE = {}
 
@@ -36,7 +37,7 @@ def _count(mask):
 
 def _plan(ranks, topo):
     if "way" in _CACHE:
-        return _CACHE["way"], _CACHE["job"]
+        return _CACHE["way"], _CACHE["jobs"]
 
     def same_chip(a, b):
         return topo.host(a) == topo.host(b) and topo.chip(a) == topo.chip(b)
@@ -47,65 +48,68 @@ def _plan(ranks, topo):
     free = [c for c in range(WORLD) if c not in ranks and any(same_chip(c, r) for r in ranks)]
     turns = {c: any(topo.mates(c, m) and topo.may_write(c, m) for m in range(WORLD)) for c in free}
 
-    kind = {}
+    kind, to = {}, {s: {} for s in ranks}
     for s in ranks:
         for d in ranks:
             if s == d:
                 continue
             if topo.may_write(s, d):
-                kind[s, d] = "near" if topo.same_plane(s, d) else "far"
+                k = "near" if topo.same_plane(s, d) else "far"
             elif any(same_chip(c, s) and topo.may_write(c, d) for c in free):
-                kind[s, d] = "t_host" if topo.host(s) == topo.host(d) else "t_rack" if same_rack(s, d) else "t_far"
+                k = "t_host" if topo.host(s) == topo.host(d) else "t_rack" if same_rack(s, d) else "t_far"
             else:
-                kind[s, d] = "x_same" if topo.chip(s) == topo.chip(d) else "x_turn"
+                k = "x_same" if topo.chip(s) == topo.chip(d) else "x_turn"
+            kind[s, d] = k
+            to[s][k] = d
 
-    fits = {
-        "t_host": lambda c, s, d: same_chip(c, s) and topo.die(c) == topo.die(s),
-        "t_far": lambda c, s, d: same_chip(c, s) and topo.die(c) == topo.die(s),
-        "t_rack": lambda c, s, d: same_chip(c, s) and topo.die(c) != topo.die(s),
-        "x_turn": lambda c, s, d: (topo.chip(c) == topo.chip(s) and not same_rack(c, s) and same_rack(c, d)
-                                   and topo.die(c) != topo.die(s)),
-        "x_same": lambda c, s, d: (topo.chip(c) == topo.chip(s) and topo.same_plane(c, s) and not turns[c]
-                                   and topo.die(c) == topo.die(s)),
+    ha = {s: [c for c in free if same_chip(c, s) and turns[c] and topo.die(c) == topo.die(s)][0] for s in ranks}
+    hb = {s: [c for c in free if same_chip(c, s) and turns[c] and topo.die(c) != topo.die(s)][0] for s in ranks}
+    relay = {
+        "near": lambda s: None,
+        "far": lambda s: None,
+        "t_far": lambda s: ha[s],
+        "t_rack": lambda s: hb[s],
+        "t_host": lambda s: hb[s],
+        "x_turn": lambda s: ha[to[s]["far"]],
+        "x_same": lambda s: hb[to[s]["near"]],
     }
-    way, job = {}, {}
-    for k in ("near", "far", "t_host", "t_far", "t_rack", "x_turn", "x_same"):
-        for (s, d), kk in sorted(kind.items()):
-            if kk != k:
-                continue
-            h = None
-            if k in fits:
-                h = [c for c in free if fits[k](c, s, d) and topo.may_write(s, c) and topo.may_write(c, d)][0]
-                free.remove(h)
-                job[h] = (s, d)
-            way[s, d] = (k, h)
-    for (s, d), (k, h) in sorted(way.items()):
-        first = d if h is None else h
-        out = _bits([topo.mask(s, x) for x in ranks if x != s and topo.may_write(s, x)][0])
-        if same_chip(first, s):
-            mine = [b for b in _bits(topo.mask(s, first)) if b not in out]
-            m1 = mine if k == "t_host" else mine[0::2] if k == "t_rack" else mine[1::2]
-        else:
-            m1 = out[0::2] if k in ("x_same", "near") else out[1::2]
-        m2 = _bits(topo.mask(h, d))[0::2] if h is not None else []
-        way[s, d] = (k, h, sum(m1), sum(m2))
-    _CACHE["way"], _CACHE["job"] = way, job
-    return way, job
+    way, jobs = {}, {}
+    for k in ("near", "far", "x_same", "t_far", "x_turn", "t_rack", "t_host"):
+        for s in ranks:
+            d = to[s][k]
+            h = relay[k](s)
+            first = d if h is None else h
+            out = _bits(topo.mask(s, to[s]["near"]))
+            if same_chip(first, s):
+                m1 = [b for b in _bits(topo.mask(s, first)) if b not in out]
+            else:
+                m1 = out[0::2] if k == "near" else out[1::2] if k == "far" else out
+            j, m2 = 0, []
+            if h is not None:
+                assert topo.may_write(s, h) and topo.may_write(h, d)
+                j = len(jobs.setdefault(h, []))
+                jobs[h].append((s, d))
+                m2 = _bits(topo.mask(h, d))[0::2]
+            way[s, d] = (k, h, j, sum(m1), sum(m2))
+    _CACHE["way"], _CACHE["jobs"] = way, jobs
+    return way, jobs
 
 
 def rank_program(g, core, T, topo):
     ranks = list(T.cores)
-    way, job = _plan(ranks, topo)
+    way, jobs = _plan(ranks, topo)
     sem = T.sem
 
-    if core in job:
-        s, d = job[core]
-        _, _, m1, m2 = way[s, d]
-        rs = T.rank_of(s)
-        rid, pid = topo.addr(d, core)
-        g.wait_ge(sem.rin, _count(m1))
-        g.remote_dma(T.land[rs], T.rly[:, :], sem["a%d" % rs], sem.sent, pid, rid, m2)
-        g.wait_ge(sem.sent, _count(m2))
+    if core in jobs:
+        sent = 0
+        for s, d in jobs[core]:
+            _, _, j, m1, m2 = way[s, d]
+            rs = T.rank_of(s)
+            rid, pid = topo.addr(d, core)
+            g.wait_ge(sem["rin%d" % j], _count(m1))
+            g.remote_dma(T.land[rs], T.rly[j], sem["a%d" % rs], sem.sent, pid, rid, m2)
+            sent += _count(m2)
+        g.wait_ge(sem.sent, sent)
         return
 
     r = T.rank_of(core)
@@ -131,9 +135,7 @@ def rank_program(g, core, T, topo):
         q.wait_ge(sem.offs, 1)
         q.wait_ge(sem.xsem, 16)
 
-    sent = 0
     for row in ROUNDS:
-        transfers = []
         for i, k in enumerate(row):
             rd = T.rank_of(to[k])
             blk = T.snd[:, rd * W:(rd + 1) * W]
@@ -142,16 +144,20 @@ def rank_program(g, core, T, topo):
                 g.vector.tensor_copy(blk, win).then_inc(sem["g%d" % rd], 1)
             else:
                 g.scalar.activation(blk, win, ActivationFunctionType.Copy).then_inc(sem["g%d" % rd], 1)
-            if k == "own":
-                continue
-            _, h, m1, _ = way[core, to[k]]
+
+    sent = 0
+    for call in CALLS:
+        transfers = []
+        for k in call:
+            rd = T.rank_of(to[k])
+            _, h, j, m1, _ = way[core, to[k]]
             g.wait_ge(sem["g%d" % rd], 1)
             first = to[k] if h is None else h
             rid, pid = topo.addr(first, core)
             transfers.append(RemoteDMATransfer(
                 dst_ids=[DstId(rid=rid, pnc=pid)], dma_engine_mask=m1,
-                remote_sem=sem["a%d" % r] if h is None else sem.rin,
-                src=blk, dst=T.land[r] if h is None else T.rly[:, :]))
+                remote_sem=sem["a%d" % r] if h is None else sem["rin%d" % j],
+                src=T.snd[:, rd * W:(rd + 1) * W], dst=T.land[r] if h is None else T.rly[j]))
             sent += _count(m1)
         g.remote_dma_fused(transfers, local_sem=sem.sent)
 
@@ -162,7 +168,7 @@ def rank_program(g, core, T, topo):
                 q.wait_ge(sem["g%d" % rs], 1)
                 src = T.snd[:, rs * W:(rs + 1) * W]
             else:
-                _, h, m1, m2 = way[frm[k], core]
+                _, h, _, m1, m2 = way[frm[k], core]
                 q.wait_ge(sem["a%d" % rs], _count(m1 if h is None else m2))
                 src = T.land[rs]
             q.dma_start(T.y[:, rs * W:(rs + 1) * W], src).then_inc(st, 16)

@@ -3,6 +3,7 @@ from concourse.mybir import AluOpType, ActivationFunctionType
 
 N, COLS, W, LP = 8, 4096, 256, 16
 LC = W // LP
+HW = W // 2
 WORLD = 512
 
 SCRATCH = {
@@ -14,15 +15,18 @@ SCRATCH = {
     "off": ("sbuf", [128, N * LC], "uint16"),
     "snd": ("sbuf", [128, N * W], "bfloat16"),
     "rly": ("dram", [3, 128, W], "bfloat16"),
+    "rlyh": ("dram", [1, 128, HW], "bfloat16"),
     "land": ("dram", [N, 128, W], "bfloat16"),
+    "landh": ("dram", [2, 128, HW], "bfloat16"),
 }
-SEMAPHORES = (["lsem", "xsem", "one", "rsel", "lfs", "mm", "offs", "rin0", "rin1", "rin2", "sent", "st1", "st2"]
+SEMAPHORES = (["lsem", "xsem", "one", "rsel", "lfs", "mm", "offs", "rin0", "rin1", "rin2", "rinh", "fa", "fb",
+               "sent", "st1", "st2"]
               + ["g%d" % i for i in range(N)] + ["a%d" % i for i in range(N)])
 
-ROUNDS = (("x_same", "t_far"), ("x_turn", "t_rack"), ("t_host", "near"), ("far", "own"))
-CALLS = (("x_same", "t_far"), ("x_turn", "t_rack"), ("t_host", "near", "far"))
-STORE_SYNC = ("x_same", "near", "t_rack", "t_host")
-STORE_SCALAR = ("t_far", "own", "far", "x_turn")
+ROUNDS = (("x_same", "t_far"), ("x_turn", "near"), ("t_rack", "far"), ("t_host", "own"))
+CALLS = (("x_same", "t_far"), ("x_turn", "near", "t_rack"), ("far_a", "far_b"), ("t_host",))
+STORE_SYNC = ("t_rack", "x_same", "t_host", "far_b")
+STORE_SCALAR = ("near", "own", "t_far", "far_a", "x_turn")
 
 _CACHE = {}
 
@@ -37,7 +41,7 @@ def _count(mask):
 
 def _plan(ranks, topo):
     if "way" in _CACHE:
-        return _CACHE["way"], _CACHE["jobs"]
+        return _CACHE["way"], _CACHE["jobs"], _CACHE["half"]
 
     def same_chip(a, b):
         return topo.host(a) == topo.host(b) and topo.chip(a) == topo.chip(b)
@@ -64,6 +68,7 @@ def _plan(ranks, topo):
 
     ha = {s: [c for c in free if same_chip(c, s) and turns[c] and topo.die(c) == topo.die(s)][0] for s in ranks}
     hb = {s: [c for c in free if same_chip(c, s) and turns[c] and topo.die(c) != topo.die(s)][0] for s in ranks}
+    hc = {s: [c for c in free if same_chip(c, s) and not turns[c] and topo.die(c) != topo.die(s)][0] for s in ranks}
     relay = {
         "near": lambda s: None,
         "far": lambda s: None,
@@ -73,7 +78,7 @@ def _plan(ranks, topo):
         "x_turn": lambda s: ha[to[s]["far"]],
         "x_same": lambda s: hb[to[s]["near"]],
     }
-    way, jobs = {}, {}
+    way, jobs, half = {}, {}, {}
     for k in ("near", "far", "x_same", "t_far", "x_turn", "t_rack", "t_host"):
         for s in ranks:
             d = to[s][k]
@@ -83,21 +88,25 @@ def _plan(ranks, topo):
             if same_chip(first, s):
                 m1 = [b for b in _bits(topo.mask(s, first)) if b not in out]
             else:
-                m1 = out[0::2] if k == "near" else out[1::2] if k == "far" else out
+                m1 = out[0::2] if k == "near" else out[1::2] if k in ("far", "x_turn") else out
             j, m2 = 0, []
             if h is not None:
                 assert topo.may_write(s, h) and topo.may_write(h, d)
                 j = len(jobs.setdefault(h, []))
                 jobs[h].append((s, d))
-                m2 = _bits(topo.mask(h, d))[0::2]
+                m2 = _bits(topo.mask(h, d))[min(j, 1)::2]
             way[s, d] = (k, h, j, sum(m1), sum(m2))
-    _CACHE["way"], _CACHE["jobs"] = way, jobs
-    return way, jobs
+            if k == "far":
+                c = hc[s]
+                assert topo.may_write(s, c) and topo.may_write(c, d)
+                half[s] = (c, sum(b for b in _bits(topo.mask(s, c)) if b not in out), sum(_bits(topo.mask(c, d))[0::2]))
+    _CACHE["way"], _CACHE["jobs"], _CACHE["half"] = way, jobs, half
+    return way, jobs, half
 
 
 def rank_program(g, core, T, topo):
     ranks = list(T.cores)
-    way, jobs = _plan(ranks, topo)
+    way, jobs, half = _plan(ranks, topo)
     sem = T.sem
 
     if core in jobs:
@@ -111,6 +120,16 @@ def rank_program(g, core, T, topo):
             sent += _count(m2)
         g.wait_ge(sem.sent, sent)
         return
+
+    for s in ranks:
+        if half[s][0] == core:
+            _, m1, m2 = half[s]
+            d = [e for e in ranks if e != s and way[s, e][0] == "far"][0]
+            rid, pid = topo.addr(d, core)
+            g.wait_ge(sem.rinh, _count(m1))
+            g.remote_dma(T.landh[1], T.rlyh[0], sem.fb, sem.sent, pid, rid, m2)
+            g.wait_ge(sem.sent, _count(m2))
+            return
 
     r = T.rank_of(core)
     if r is None:
@@ -149,20 +168,40 @@ def rank_program(g, core, T, topo):
     for call in CALLS:
         transfers = []
         for k in call:
-            rd = T.rank_of(to[k])
-            _, h, j, m1, _ = way[core, to[k]]
+            if k in ("far_a", "far_b"):
+                d = to["far"]
+                rd = T.rank_of(d)
+                if k == "far_a":
+                    first, m1, rsem, dst, lo = d, way[core, d][3], sem.fa, T.landh[0], rd * W
+                else:
+                    first, m1, rsem, dst, lo = half[core][0], half[core][1], sem.rinh, T.rlyh[0], rd * W + HW
+                src = T.snd[:, lo:lo + HW]
+            else:
+                rd = T.rank_of(to[k])
+                _, h, j, m1, _ = way[core, to[k]]
+                first = to[k] if h is None else h
+                rsem = sem["a%d" % r] if h is None else sem["rin%d" % j]
+                dst = T.land[r] if h is None else T.rly[j]
+                src = T.snd[:, rd * W:(rd + 1) * W]
             g.wait_ge(sem["g%d" % rd], 1)
-            first = to[k] if h is None else h
             rid, pid = topo.addr(first, core)
-            transfers.append(RemoteDMATransfer(
-                dst_ids=[DstId(rid=rid, pnc=pid)], dma_engine_mask=m1,
-                remote_sem=sem["a%d" % r] if h is None else sem["rin%d" % j],
-                src=T.snd[:, rd * W:(rd + 1) * W], dst=T.land[r] if h is None else T.rly[j]))
+            transfers.append(RemoteDMATransfer(dst_ids=[DstId(rid=rid, pnc=pid)], dma_engine_mask=m1, remote_sem=rsem,
+                                               src=src, dst=dst))
             sent += _count(m1)
         g.remote_dma_fused(transfers, local_sem=sem.sent)
 
     for q, order, st in ((g.sync, STORE_SYNC, sem.st1), (g.scalar, STORE_SCALAR, sem.st2)):
         for k in order:
+            if k in ("far_a", "far_b"):
+                s = frm["far"]
+                rs = T.rank_of(s)
+                if k == "far_a":
+                    q.wait_ge(sem.fa, _count(way[s, core][3]))
+                    q.dma_start(T.y[:, rs * W:rs * W + HW], T.landh[0]).then_inc(st, 16)
+                else:
+                    q.wait_ge(sem.fb, _count(half[s][2]))
+                    q.dma_start(T.y[:, rs * W + HW:(rs + 1) * W], T.landh[1]).then_inc(st, 16)
+                continue
             rs = T.rank_of(frm[k])
             if k == "own":
                 q.wait_ge(sem["g%d" % rs], 1)

from concourse.bass import DstId, RemoteDMATransfer
from concourse.mybir import AluOpType, ActivationFunctionType

N, COLS, W, LP = 8, 4096, 256, 16
LC = W // LP
HW = W // 2
WORLD = 512

SCRATCH = {
    "xs": ("sbuf", [128, COLS], "bfloat16"),
    "li": ("sbuf", [128, N * LC], "int32"),
    "lf": ("sbuf", [128, N * LC], "float32"),
    "rep": ("sbuf", [128, 128], "float32"),
    "ps": ("psum", [128, N * LC], "float32"),
    "off": ("sbuf", [128, N * LC], "uint16"),
    "snd": ("sbuf", [128, N * W], "bfloat16"),
    "rly": ("dram", [3, 128, W], "bfloat16"),
    "rlyh": ("dram", [1, 128, HW], "bfloat16"),
    "land": ("dram", [N, 128, W], "bfloat16"),
    "landh": ("dram", [2, 128, HW], "bfloat16"),
}
SEMAPHORES = (["lsem", "xsem", "one", "rsel", "lfs", "mm", "offs", "rin0", "rin1", "rin2", "rinh", "fa", "fb",
               "sent", "st1", "st2"]
              + ["g%d" % i for i in range(N)] + ["a%d" % i for i in range(N)])

ROUNDS = (("x_same", "t_far"), ("x_turn", "near"), ("t_rack", "far"), ("t_host", "own"))
CALLS = (("x_same", "t_far"), ("x_turn", "near", "t_rack"), ("far_a", "far_b"), ("t_host",))
STORE_SYNC = ("t_rack", "x_same", "t_host", "far_b")
STORE_SCALAR = ("near", "own", "t_far", "far_a", "x_turn")

_CACHE = {}


def _bits(mask):
    return [1 << i for i in range(mask.bit_length()) if mask >> i & 1]


def _count(mask):
    return len(_bits(mask))


def _plan(ranks, topo):
    if "way" in _CACHE:
        return _CACHE["way"], _CACHE["jobs"], _CACHE["half"]

    def same_chip(a, b):
        return topo.host(a) == topo.host(b) and topo.chip(a) == topo.chip(b)

    def same_rack(a, b):
        return topo.rack(topo.host(a)) == topo.rack(topo.host(b))

    free = [c for c in range(WORLD) if c not in ranks and any(same_chip(c, r) for r in ranks)]
    turns = {c: any(topo.mates(c, m) and topo.may_write(c, m) for m in range(WORLD)) for c in free}

    kind, to = {}, {s: {} for s in ranks}
    for s in ranks:
        for d in ranks:
            if s == d:
                continue
            if topo.may_write(s, d):
                k = "near" if topo.same_plane(s, d) else "far"
            elif any(same_chip(c, s) and topo.may_write(c, d) for c in free):
                k = "t_host" if topo.host(s) == topo.host(d) else "t_rack" if same_rack(s, d) else "t_far"
            else:
                k = "x_same" if topo.chip(s) == topo.chip(d) else "x_turn"
            kind[s, d] = k
            to[s][k] = d

    ha = {s: [c for c in free if same_chip(c, s) and turns[c] and topo.die(c) == topo.die(s)][0] for s in ranks}
    hb = {s: [c for c in free if same_chip(c, s) and turns[c] and topo.die(c) != topo.die(s)][0] for s in ranks}
    hc = {s: [c for c in free if same_chip(c, s) and not turns[c] and topo.die(c) != topo.die(s)][0] for s in ranks}
    relay = {
        "near": lambda s: None,
        "far": lambda s: None,
        "t_far": lambda s: ha[s],
        "t_rack": lambda s: hb[s],
        "t_host": lambda s: hb[s],
        "x_turn": lambda s: ha[to[s]["far"]],
        "x_same": lambda s: hb[to[s]["near"]],
    }
    way, jobs, half = {}, {}, {}
    for k in ("near", "far", "x_same", "t_far", "x_turn", "t_rack", "t_host"):
        for s in ranks:
            d = to[s][k]
            h = relay[k](s)
            first = d if h is None else h
            out = _bits(topo.mask(s, to[s]["near"]))
            if same_chip(first, s):
                m1 = [b for b in _bits(topo.mask(s, first)) if b not in out]
            else:
                m1 = out[0::2] if k == "near" else out[1::2] if k in ("far", "x_turn") else out
            j, m2 = 0, []
            if h is not None:
                assert topo.may_write(s, h) and topo.may_write(h, d)
                j = len(jobs.setdefault(h, []))
                jobs[h].append((s, d))
                m2 = _bits(topo.mask(h, d))[min(j, 1)::2]
            way[s, d] = (k, h, j, sum(m1), sum(m2))
            if k == "far":
                c = hc[s]
                assert topo.may_write(s, c) and topo.may_write(c, d)
                half[s] = (c, sum(b for b in _bits(topo.mask(s, c)) if b not in out), sum(_bits(topo.mask(c, d))[0::2]))
    _CACHE["way"], _CACHE["jobs"], _CACHE["half"] = way, jobs, half
    return way, jobs, half


def rank_program(g, core, T, topo):
    ranks = list(T.cores)
    way, jobs, half = _plan(ranks, topo)
    sem = T.sem

    if core in jobs:
        sent = 0
        for s, d in jobs[core]:
            _, _, j, m1, m2 = way[s, d]
            rs = T.rank_of(s)
            rid, pid = topo.addr(d, core)
            g.wait_ge(sem["rin%d" % j], _count(m1))
            g.remote_dma(T.land[rs], T.rly[j], sem["a%d" % rs], sem.sent, pid, rid, m2)
            sent += _count(m2)
        g.wait_ge(sem.sent, sent)
        return

    for s in ranks:
        if half[s][0] == core:
            _, m1, m2 = half[s]
            d = [e for e in ranks if e != s and way[s, e][0] == "far"][0]
            rid, pid = topo.addr(d, core)
            g.wait_ge(sem.rinh, _count(m1))
            g.remote_dma(T.landh[1], T.rlyh[0], sem.fb, sem.sent, pid, rid, m2)
            g.wait_ge(sem.sent, _count(m2))
            return

    r = T.rank_of(core)
    if r is None:
        return
    to = {way[core, d][0]: d for d in ranks if d != core}
    frm = {way[s, core][0]: s for s in ranks if s != core}
    to["own"] = frm["own"] = core

    g.sync.dma_start(T.li[0:LP, :], T.l[:, :]).then_inc(sem.lsem, 16)
    g.sync.dma_start(T.xs[:, :], T.x[:, :]).then_inc(sem.xsem, 16)
    g.vector.memset(T.rep[0:LP, :], 1.0).then_inc(sem.one, 1)
    g.wait_ge(sem.one, 1)
    g.affine_select(T.rep[0:LP, :], T.rep[0:LP, :], [[0, 128 // LP], [-1, LP]], AluOpType.is_equal, 0.0, 0, 1).then_inc(sem.rsel, 1)
    g.vector.wait_ge(sem.lsem, 16)
    g.vector.tensor_copy(T.lf[0:LP, :], T.li[0:LP, :]).then_inc(sem.lfs, 1)
    g.tensor.wait_ge(sem.rsel, 1)
    g.tensor.wait_ge(sem.lfs, 1)
    g.tensor.matmul(T.ps[:, :], T.rep[0:LP, :], T.lf[0:LP, :], True, True).then_inc(sem.mm, 1)
    g.vector.wait_ge(sem.mm, 1)
    g.vector.tensor_copy(T.off[:, :], T.ps[:, :]).then_inc(sem.offs, 1)
    for q in (g.vector, g.scalar):
        q.wait_ge(sem.offs, 1)
        q.wait_ge(sem.xsem, 16)

    for row in ROUNDS:
        for i, k in enumerate(row):
            rd = T.rank_of(to[k])
            blk = T.snd[:, rd * W:(rd + 1) * W]
            win = T.xs[:, 0:COLS].indirect(T.off[:, rd * LC:(rd + 1) * LC])
            if i == 0:
                g.vector.tensor_copy(blk, win).then_inc(sem["g%d" % rd], 1)
            else:
                g.scalar.activation(blk, win, ActivationFunctionType.Copy).then_inc(sem["g%d" % rd], 1)

    sent = 0
    for call in CALLS:
        transfers = []
        for k in call:
            if k in ("far_a", "far_b"):
                d = to["far"]
                rd = T.rank_of(d)
                if k == "far_a":
                    first, m1, rsem, dst, lo = d, way[core, d][3], sem.fa, T.landh[0], rd * W
                else:
                    first, m1, rsem, dst, lo = half[core][0], half[core][1], sem.rinh, T.rlyh[0], rd * W + HW
                src = T.snd[:, lo:lo + HW]
            else:
                rd = T.rank_of(to[k])
                _, h, j, m1, _ = way[core, to[k]]
                first = to[k] if h is None else h
                rsem = sem["a%d" % r] if h is None else sem["rin%d" % j]
                dst = T.land[r] if h is None else T.rly[j]
                src = T.snd[:, rd * W:(rd + 1) * W]
            g.wait_ge(sem["g%d" % rd], 1)
            rid, pid = topo.addr(first, core)
            transfers.append(RemoteDMATransfer(dst_ids=[DstId(rid=rid, pnc=pid)], dma_engine_mask=m1, remote_sem=rsem,
                                               src=src, dst=dst))
            sent += _count(m1)
        g.remote_dma_fused(transfers, local_sem=sem.sent)

    for q, order, st in ((g.sync, STORE_SYNC, sem.st1), (g.scalar, STORE_SCALAR, sem.st2)):
        for k in order:
            if k in ("far_a", "far_b"):
                s = frm["far"]
                rs = T.rank_of(s)
                if k == "far_a":
                    q.wait_ge(sem.fa, _count(way[s, core][3]))
                    q.dma_start(T.y[:, rs * W:rs * W + HW], T.landh[0]).then_inc(st, 16)
                else:
                    q.wait_ge(sem.fb, _count(half[s][2]))
                    q.dma_start(T.y[:, rs * W + HW:(rs + 1) * W], T.landh[1]).then_inc(st, 16)
                continue
            rs = T.rank_of(frm[k])
            if k == "own":
                q.wait_ge(sem["g%d" % rs], 1)
                src = T.snd[:, rs * W:(rs + 1) * W]
            else:
                _, h, _, m1, m2 = way[frm[k], core]
                q.wait_ge(sem["a%d" % rs], _count(m1 if h is None else m2))
                src = T.land[rs]
            q.dma_start(T.y[:, rs * W:(rs + 1) * W], src).then_inc(st, 16)
        q.wait_ge(st, 16 * len(order))
    g.wait_ge(sem.sent, sent)
